import numpy as np
import ml_dtypes


def mxq(x, axis, fmt="e4m3"):
    dtype, down = {"e4m3": (ml_dtypes.float8_e4m3fn, 7), "e5m2": (ml_dtypes.float8_e5m2, 14)}[fmt]
    v = np.moveaxis(np.asarray(x, np.float32).astype(ml_dtypes.bfloat16).astype(np.float64), axis, -1)
    blocks = v.reshape(v.shape[:-1] + (-1, 32))
    amax = np.abs(blocks).max(-1, keepdims=True)
    byte = np.maximum(np.where(amax > 0, np.frexp(amax)[1] - 1 + 127, 0) - down, 1)
    scale = np.exp2(byte - 127.0)
    codes = (blocks / scale).astype(np.float32).astype(dtype).astype(np.float64)
    return np.moveaxis((codes * scale).reshape(v.shape), -1, axis)


WIDE = False


def mx_kscale(k):
    if not WIDE:
        return np.ones(k)
    levels = np.array([30, -30])
    if k % 512:
        return np.exp2(np.random.permutation(np.resize(levels, k // 32))).repeat(32)
    a = np.empty((k // 512, 16))
    for p in range(k // 512):
        a[p, :8] = np.random.permutation(np.resize(levels, 8))
        for g in range(8):
            far = levels[np.abs(levels - a[p, g]) >= 10]
            a[p, g + 8] = far[np.random.randint(len(far))]
    return np.exp2(a.ravel()).repeat(32)


def f64(x):
    return np.asarray(x).astype(np.float64)


def striped(idx):
    return np.tile(np.asarray(idx).reshape(-1, 16).T, (8, 1)).astype(np.uint16)


def unstriped(offs):
    return offs[:16].T.reshape(-1).astype(np.int64)


E2M1 = np.array([0.0, 0.5, 1.0, 1.5, 2.0, 3.0, 4.0, 6.0, -0.0, -0.5, -1.0, -1.5, -2.0, -3.0, -4.0, -6.0])


def pack_weight(w, fmt):
    k, n = w.shape
    w = f64(np.asarray(w, np.float32).astype(ml_dtypes.bfloat16)).reshape(k // 32, 32, n)
    amax = np.abs(w).max(1)
    if fmt in ("e4m3", "e5m2"):
        byte = np.frexp(amax)[1] - 1 + 127 - (7 if fmt == "e4m3" else 14)
    else:
        mant, ex = np.frexp(amax / 6.0)
        byte = np.where(mant > 0.5, ex, ex - 1) + 127
    byte = np.clip(np.where(amax > 0, byte, 1), 1, 254)
    scaled = (w * np.exp2(127.0 - byte)[:, None, :]).reshape(k, n).astype(np.float32)
    by_word = np.ascontiguousarray(scaled.reshape(k // 512, 128, 4, n).transpose(0, 1, 3, 2))
    if fmt in ("e4m3", "e5m2"):
        words = by_word.astype(ml_dtypes.float8_e4m3fn if fmt == "e4m3" else ml_dtypes.float8_e5m2).view(np.uint8)
    else:
        c = by_word.astype(ml_dtypes.float4_e2m1fn).view(np.uint8) & 0xF
        words = (c[..., 0::2] | (c[..., 1::2] << 4)).reshape(k // 512, 128, 2 * n)
    return np.ascontiguousarray(words), np.ascontiguousarray(byte.astype(np.uint8).reshape(k // 512, 16, n))


def unpack_weight(words, scales, fmt):
    g, _, n = scales.shape
    words = np.ascontiguousarray(words).reshape(g, 128, n, -1)
    if fmt in ("e4m3", "e5m2"):
        vals = words.view(ml_dtypes.float8_e4m3fn if fmt == "e4m3" else ml_dtypes.float8_e5m2).astype(np.float64)
    else:
        nib = np.empty((g, 128, n, 4), np.uint8)
        nib[..., 0::2] = words & 0xF
        nib[..., 1::2] = words >> 4
        vals = E2M1[nib]
    vals = vals * np.repeat(np.exp2(scales.astype(np.float64) - 127.0), 8, axis=1)[..., None]
    return vals.transpose(0, 1, 3, 2).reshape(g * 512, n)


K, F, T, Z, J, R, O, N = 512, 512, 1024, 1024, 256, 512, 128, 256


def setup_inputs():
    n = np.random.standard_normal
    idx = np.random.permutation(T)[:J]
    idx2 = np.random.permutation(Z)[:J]
    idx3 = np.random.permutation(J)[:O]
    idx4 = np.random.permutation(J)[:O]
    idx5 = np.random.permutation(T)[:O]
    fk = mx_kscale(K)
    fr = mx_kscale(R)
    ff = mx_kscale(F)
    xtp = pack_weight(n((K, T)) / fk[:, None], "e5m2")
    wp = pack_weight(n((K, R)) * 1 / np.sqrt(K) * fk[:, None] * fr, "e2m1")
    xop = pack_weight(n((F, Z)) / ff[:, None], "e4m3")
    w2p = pack_weight(n((F, R)) * 1 / np.sqrt(F) * ff[:, None] * fr, "e2m1")
    wbp = pack_weight(n((R, N)) * 1 / np.sqrt(R) / fr[:, None], "e2m1")
    wsp = pack_weight(n((K, N)) * 1 / np.sqrt(K) * fk[:, None], "e2m1")
    return {
        "xt_words": xtp[0],
        "xt_scales": xtp[1],
        "w_words": wp[0],
        "w_scales": wp[1],
        "xo_words": xop[0],
        "xo_scales": xop[1],
        "w2_words": w2p[0],
        "w2_scales": w2p[1],
        "sa": (np.random.uniform(0.5, 1.6, (R, 1))).astype(np.float32),
        "sb": (np.random.uniform(0.5, 1.6, (R, 1))).astype(np.float32),
        "wb_words": wbp[0],
        "wb_scales": wbp[1],
        "ws_words": wsp[0],
        "ws_scales": wsp[1],
        "offs": striped(idx),
        "offs2": striped(idx2),
        "offs3": striped(idx3),
        "offs4": striped(idx4),
        "offs5": striped(idx5),
    }


def reference(xt_words, xt_scales, w_words, w_scales, xo_words, xo_scales, w2_words, w2_scales, sa, sb, wb_words, wb_scales, ws_words, ws_scales, offs, offs2, offs3, offs4, offs5):
    idx = unstriped(offs)
    idx2 = unstriped(offs2)
    idx3 = unstriped(offs3)
    idx4 = unstriped(offs4)
    idx5 = unstriped(offs5)
    xtu = unpack_weight(xt_words, xt_scales, "e5m2")
    wu = unpack_weight(w_words, w_scales, "e2m1")
    xou = unpack_weight(xo_words, xo_scales, "e4m3")
    w2u = unpack_weight(w2_words, w2_scales, "e2m1")
    wbu = unpack_weight(wb_words, wb_scales, "e2m1")
    wsu = unpack_weight(ws_words, ws_scales, "e2m1")
    xtidxg = xtu[:, idx]
    a = wu.T @ xtidxg
    xoidx2g = xou[:, idx2]
    b = w2u.T @ xoidx2g
    hid = np.abs(a[:, idx3] * f64(sa) - b[:, idx4] * f64(sb))
    hidq = mxq(hid, 0, "e4m3")
    xtidx5g = xtu[:, idx5]
    y = wbu.T @ hidq + wsu.T @ xtidx5g
    return y

@@ -1,0 +1,200 @@
+from contextlib import ExitStack
+
+import concourse.mybir as mybir
+
+K, T, J, R, O, N = 512, 1024, 256, 512, 128, 256
+FLOPS = 2 * K * R * J * 2 + 2 * R * N * O * 2
+
+F32 = mybir.dt.float32
+BF16 = mybir.dt.bfloat16
+I32 = mybir.dt.int32
+U32 = mybir.dt.uint32
+U16 = mybir.dt.uint16
+U8 = mybir.dt.uint8
+E4M3 = mybir.dt.float8_e4m3fn_x4
+E5M2 = mybir.dt.float8_e5m2_x4
+E2M1 = mybir.dt.float4_e2m1fn_x4
+ALU = mybir.AluOpType
+ACT = mybir.ActivationFunctionType
+P = 128
+
+
+def tile_list_weighedboth_twotab_further_plain_kernel(tc, xt_words, xt_scales, w_words, w_scales, xo_words, xo_scales, w2_words, w2_scales, sa, sb, wb_words, wb_scales, ws_words, ws_scales, offs, offs2, offs3, offs4, offs5, out):
+    nc = tc.nc
+    with ExitStack() as ctx:
+        sbuf = ctx.enter_context(tc.tile_pool(name="sbuf", bufs=1))
+        psum = ctx.enter_context(tc.psum_pool(name="psum", bufs=1))
+
+        def tile(name, shape, dtype):
+            return sbuf.tile(shape, dtype, name=name, align_bytes=64)
+
+        lists = {}
+
+        def load_list(name, src):
+            lists[name] = tile(name, list(src.shape), U16)
+            nc.sync.dma_start(lists[name][:], src)
+
+        def load_words(queue, name, src, dtype):
+            words = tile(name, [P, src.shape[1] * 4 // {U32: 4, U8: 1}[dtype]], dtype)
+            queue.dma_start(words[:].bitcast(I32), src)
+            return words
+
+        def load_plane(queue, plane, src):
+            for q in range(4):
+                queue.dma_start(plane[32 * q : 32 * q + 4, :].bitcast(I32), src[0, 4 * q : 4 * q + 4, :].bitcast(I32))
+
+        def load_staged(queue, stage, src):
+            queue.dma_start(
+                stage[0:4, :].bitcast(I32).rearrange("r (q c) -> r q c", q=4),
+                src[0].bitcast(I32).rearrange("(q r) c -> r q c", q=4),
+            )
+
+        def spread(pairs):
+            for q in range(4):
+                for plane, stage in pairs:
+                    c = plane.shape[1] // 4
+                    nc.vector.tensor_copy(plane[32 * q : 32 * q + 4, :].bitcast(I32), stage[:].bitcast(I32)[:, q * c : (q + 1) * c])
+
+        def deal_scales(name, plane):
+            dealt = tile(name, [P, R], U8)
+            nc.vector.tensor_copy(
+                dealt[:].rearrange("p (t q) -> p t q", t=4),
+                plane[:].rearrange("p (q t) -> p t q", t=4),
+            )
+            return dealt
+
+        def deal_words(name, raw):
+            dealt = tile(name, [P, 2 * R], U8)
+            nc.scalar.copy(
+                dealt[:].bitcast(U16).rearrange("p (t q) -> p t q", t=4),
+                raw[:].bitcast(U16).rearrange("p (q t) -> p t q", t=4),
+            )
+            return dealt
+
+        def gather(name, table, offsets, dtype):
+            picked = tile(name, [P, 16 * offsets.shape[1]], dtype)
+            nc.vector.tensor_copy(picked[:], table[:].indirect(offsets[:]))
+            return picked
+
+        xt_plane = tile("xt_plane", [P, T], U8)
+        xo_plane = tile("xo_plane", [P, T], U8)
+        w_plane = tile("w_plane", [P, R], U8)
+        w2_plane = tile("w2_plane", [P, R], U8)
+        xt_stage = tile("xt_stage", [4, 4 * T], U8)
+        xo_stage = tile("xo_stage", [4, 4 * T], U8)
+        w_stage = tile("w_stage", [4, 4 * R], U8)
+        w2_stage = tile("w2_stage", [4, 4 * R], U8)
+        ws_plane = tile("ws_plane", [P, N], U8)
+        wb_plane = tile("wb_plane", [P, N], U8)
+        for plane in (xt_plane, w_plane, xo_plane, w2_plane, ws_plane, wb_plane):
+            nc.vector.memset(plane[:].bitcast(I32), 0)
+
+        table_view = "p c t -> p (c t)"
+        load_staged(nc.sync, xt_stage, xt_scales)
+        w_raw = load_words(nc.scalar, "w_raw", w_words[0].bitcast(I32), U8)
+        load_staged(nc.sync, w_stage, w_scales)
+        xt_tab = load_words(nc.scalar, "xt_tab", xt_words[0].rearrange(table_view).bitcast(I32), U32)
+        load_list("offs", offs)
+        w2_raw = load_words(nc.scalar, "w2_raw", w2_words[0].bitcast(I32), U8)
+        load_staged(nc.sync, xo_stage, xo_scales)
+        xo_tab = load_words(nc.scalar, "xo_tab", xo_words[0].rearrange(table_view).bitcast(I32), U32)
+        load_staged(nc.sync, w2_stage, w2_scales)
+        sa_sb = tile("sa_sb", [P, 4], F32)
+        nc.gpsimd.dma_start(sa_sb[:], sa.rearrange("(p t) o -> p (t o)", t=4))
+        load_list("offs2", offs2)
+        load_list("offs3", offs3)
+        sb_sb = tile("sb_sb", [P, 4], F32)
+        nc.gpsimd.dma_start(sb_sb[:], sb.rearrange("(p t) o -> p (t o)", t=4))
+        load_list("offs4", offs4)
+        load_list("offs5", offs5)
+        ws_w = load_words(nc.gpsimd, "ws_w", ws_words[0].bitcast(I32), U8)
+        wb_w = load_words(nc.gpsimd, "wb_w", wb_words[0].bitcast(I32), U8)
+        load_plane(nc.sync, ws_plane, ws_scales)
+        load_plane(nc.sync, wb_plane, wb_scales)
+
+        def first_stage(bank0, weights, weight_scales, words, scales, fmt):
+            banks = []
+            for t in range(4):
+                bank = psum.tile([P, J], F32, name="bank%d" % (bank0 + t))
+                nc.tensor.matmul_mx(
+                    out=bank[:],
+                    lhsT=weights[:, 2 * P * t : 2 * P * (t + 1)].bitcast(E2M1),
+                    lhsT_scale=weight_scales[:, P * t : P * (t + 1)],
+                    rhs=words[:].bitcast(fmt),
+                    rhs_scale=scales[:],
+                    start=True,
+                    stop=True,
+                )
+                banks.append(bank)
+            return banks
+
+        w_dealt = deal_words("w_dealt", w_raw)
+        spread([(xt_plane, xt_stage), (w_plane, w_stage)])
+        w_sc = deal_scales("w_sc", w_plane)
+        a_scales = gather("a_scales", xt_plane, lists["offs"], U8)
+        a_words = gather("a_words", xt_tab, lists["offs"], U32)
+        a_banks = first_stage(0, w_dealt, w_sc, a_words, a_scales, E5M2)
+
+        w2_dealt = deal_words("w2_dealt", w2_raw)
+        spread([(xo_plane, xo_stage), (w2_plane, w2_stage)])
+        w2_sc = deal_scales("w2_sc", w2_plane)
+        b_scales = gather("b_scales", xo_plane, lists["offs2"], U8)
+        b_words = gather("b_words", xo_tab, lists["offs2"], U32)
+        b_banks = first_stage(4, w2_dealt, w2_sc, b_words, b_scales, E4M3)
+
+        a_picked = tile("a_picked", [P, 4, O], F32)
+        b_picked = tile("b_picked", [P, 4, O], F32)
+        diff = tile("diff", [P, 4, O], F32)
+        for t in range(4):
+            rows = tile("a_rows%d" % t, [P, J], F32)
+            nc.scalar.activation(rows[:], a_banks[t][:], ACT.Copy)
+            nc.scalar.activation(a_picked[:, t, :], rows[:].indirect(lists["offs3"][:]), ACT.Copy, scale=sa_sb[:, t : t + 1])
+
+        s_scales = gather("s_scales", xt_plane, lists["offs5"], U8)
+        for t in range(4):
+            rows = tile("b_rows%d" % t, [P, J], F32)
+            nc.vector.tensor_copy(rows[:], b_banks[t][:])
+            nc.scalar.activation(b_picked[:, t, :], rows[:].indirect(lists["offs4"][:]), ACT.Copy, scale=sb_sb[:, t : t + 1])
+        s_words = gather("s_words", xt_tab, lists["offs5"], U32)
+        for t in range(4):
+            nc.vector.tensor_tensor(diff[:, t, :], a_picked[:, t, :], b_picked[:, t, :], ALU.subtract)
+
+        y_banks = []
+        for h in range(2):
+            bank = psum.tile([P, O], F32, name="bank%d" % h)
+            nc.tensor.matmul_mx(
+                out=bank[:],
+                lhsT=ws_w[:, 2 * P * h : 2 * P * (h + 1)].bitcast(E2M1),
+                lhsT_scale=ws_plane[:, P * h : P * (h + 1)],
+                rhs=s_words[:].bitcast(E5M2),
+                rhs_scale=s_scales[:],
+                start=True,
+                stop=False,
+            )
+            y_banks.append(bank)
+
+        hid = tile("hid", [P, O, 4], BF16)
+        woven = diff[:].rearrange("p t o -> p o t")
+        half = O // 2
+        nc.scalar.activation(hid[:, 0:half, :], woven[:, 0:half, :], ACT.Abs)
+        nc.vector.scalar_tensor_tensor(hid[:, half:O, :], woven[:, half:O, :], -1.0, woven[:, half:O, :], ALU.mult, ALU.max)
+        hid_words = tile("hid_words", [P, O], U32)
+        hid_scales = tile("hid_scales", [P, O], U8)
+        nc.vector.quantize_mx(out=hid_words[:].bitcast(E4M3), scales=hid_scales[:], in_=hid[:].rearrange("p o t -> p (o t)"))
+
+        for h in range(2):
+            nc.tensor.matmul_mx(
+                out=y_banks[h][:],
+                lhsT=wb_w[:, 2 * P * h : 2 * P * (h + 1)].bitcast(E2M1),
+                lhsT_scale=wb_plane[:, P * h : P * (h + 1)],
+                rhs=hid_words[:].bitcast(E4M3),
+                rhs_scale=hid_scales[:],
+                start=False,
+                stop=True,
+            )
+        y0 = tile("y0", [P, O], F32)
+        y1 = tile("y1", [P, O], F32)
+        nc.vector.tensor_copy(y0[:], y_banks[0][:])
+        nc.sync.dma_start(out[0:P, :], y0[:])
+        nc.scalar.copy(y1[:], y_banks[1][:])
+        nc.scalar.dma_start(out[P : 2 * P, :], y1[:])

@@ -25,8 +25,12 @@ def tile_list_weighedboth_twotab_further_plain_kernel(tc, xt_words, xt_scales, w
         sbuf = ctx.enter_context(tc.tile_pool(name="sbuf", bufs=1))
         psum = ctx.enter_context(tc.psum_pool(name="psum", bufs=1))
 
-        def tile(name, shape, dtype):
-            return sbuf.tile(shape, dtype, name=name, align_bytes=64)
+        reused = ctx.enter_context(tc.tile_pool(name="reused", bufs=1))
+
+        def tile(name, shape, dtype, offset=None):
+            if offset is None:
+                return sbuf.tile(shape, dtype, name=name, align_bytes=64)
+            return reused.tile(shape, dtype, name=name, align_bytes=64, offset=offset)
 
         lists = {}
 
@@ -45,21 +49,15 @@ def tile_list_weighedboth_twotab_further_plain_kernel(tc, xt_words, xt_scales, w
 
         def load_staged(queue, stage, src):
             queue.dma_start(
-                stage[0:4, :].bitcast(I32).rearrange("r (q c) -> r q c", q=4),
+                stage,
                 src[0].bitcast(I32).rearrange("(q r) c -> r q c", q=4),
             )
-
-        def spread(pairs):
-            for q in range(4):
-                for plane, stage in pairs:
-                    c = plane.shape[1] // 4
-                    nc.vector.tensor_copy(plane[32 * q : 32 * q + 4, :].bitcast(I32), stage[:].bitcast(I32)[:, q * c : (q + 1) * c])
 
         def deal_scales(name, plane):
             dealt = tile(name, [P, R], U8)
             nc.vector.tensor_copy(
                 dealt[:].rearrange("p (t q) -> p t q", t=4),
-                plane[:].rearrange("p (q t) -> p t q", t=4),
+                plane.rearrange("p (q t) -> p t q", t=4),
             )
             return dealt
 
@@ -71,40 +69,39 @@ def tile_list_weighedboth_twotab_further_plain_kernel(tc, xt_words, xt_scales, w
             )
             return dealt
 
-        def gather(name, table, offsets, dtype):
-            picked = tile(name, [P, 16 * offsets.shape[1]], dtype)
+        def gather(name, table, offsets, dtype, offset=None):
+            picked = tile(name, [P, 16 * offsets.shape[1]], dtype, offset)
             nc.vector.tensor_copy(picked[:], table[:].indirect(offsets[:]))
             return picked
 
         xt_plane = tile("xt_plane", [P, T], U8)
         xo_plane = tile("xo_plane", [P, T], U8)
-        w_plane = tile("w_plane", [P, R], U8)
-        w2_plane = tile("w2_plane", [P, R], U8)
-        xt_stage = tile("xt_stage", [4, 4 * T], U8)
-        xo_stage = tile("xo_stage", [4, 4 * T], U8)
-        w_stage = tile("w_stage", [4, 4 * R], U8)
-        w2_stage = tile("w2_stage", [4, 4 * R], U8)
+        w_stage = tile("w_stage", [4, 4, 2 * R // 4], I32)
+        w_planes = tile("w_planes", [P, 2, 2 * R // 4], I32)
         ws_plane = tile("ws_plane", [P, N], U8)
         wb_plane = tile("wb_plane", [P, N], U8)
-        for plane in (xt_plane, w_plane, xo_plane, w2_plane, ws_plane, wb_plane):
+        nc.gpsimd.memset(xt_plane[:].bitcast(I32), 0)
+        nc.vector.memset(xo_plane[:].bitcast(I32), 0)
+        nc.vector.memset(w_planes[0:64], 0)
+        for plane in (ws_plane, wb_plane):
             nc.vector.memset(plane[:].bitcast(I32), 0)
 
         table_view = "p c t -> p (c t)"
-        load_staged(nc.sync, xt_stage, xt_scales)
-        w_raw = load_words(nc.scalar, "w_raw", w_words[0].bitcast(I32), U8)
-        load_staged(nc.sync, w_stage, w_scales)
-        xt_tab = load_words(nc.scalar, "xt_tab", xt_words[0].rearrange(table_view).bitcast(I32), U32)
         load_list("offs", offs)
-        w2_raw = load_words(nc.scalar, "w2_raw", w2_words[0].bitcast(I32), U8)
-        load_staged(nc.sync, xo_stage, xo_scales)
-        xo_tab = load_words(nc.scalar, "xo_tab", xo_words[0].rearrange(table_view).bitcast(I32), U32)
-        load_staged(nc.sync, w2_stage, w2_scales)
-        sa_sb = tile("sa_sb", [P, 4], F32)
-        nc.gpsimd.dma_start(sa_sb[:], sa.rearrange("(p t) o -> p (t o)", t=4))
+        load_staged(nc.sync, w_stage[:, :, 0 : R // 4], w_scales)
+        load_staged(nc.sync, w_stage[:, :, R // 4 : R // 2], w2_scales)
+        load_plane(nc.sync, xt_plane, xt_scales)
+        xt_tab = load_words(nc.sync, "xt_tab", xt_words[0].rearrange(table_view).bitcast(I32), U32)
+        xo_tab = load_words(nc.sync, "xo_tab", xo_words[0].rearrange(table_view).bitcast(I32), U32)
+        w_raw = load_words(nc.gpsimd, "w_raw", w_words[0].bitcast(I32), U8)
+        w2_raw = load_words(nc.gpsimd, "w2_raw", w2_words[0].bitcast(I32), U8)
         load_list("offs2", offs2)
         load_list("offs3", offs3)
+        load_plane(nc.sync, xo_plane, xo_scales)
+        sa_sb = tile("sa_sb", [P, 4], F32)
+        nc.sync.dma_start(sa_sb[:], sa.rearrange("(p t) o -> p (t o)", t=4))
         sb_sb = tile("sb_sb", [P, 4], F32)
-        nc.gpsimd.dma_start(sb_sb[:], sb.rearrange("(p t) o -> p (t o)", t=4))
+        nc.sync.dma_start(sb_sb[:], sb.rearrange("(p t) o -> p (t o)", t=4))
         load_list("offs4", offs4)
         load_list("offs5", offs5)
         ws_w = load_words(nc.gpsimd, "ws_w", ws_words[0].bitcast(I32), U8)
@@ -129,15 +126,17 @@ def tile_list_weighedboth_twotab_further_plain_kernel(tc, xt_words, xt_scales, w
             return banks
 
         w_dealt = deal_words("w_dealt", w_raw)
-        spread([(xt_plane, xt_stage), (w_plane, w_stage)])
-        w_sc = deal_scales("w_sc", w_plane)
+        nc.vector.tensor_copy(w_planes[0:4], w_stage[:, 0:4:2, :])
+        nc.vector.tensor_copy(w_planes[32:36].rearrange("p a c -> p (a c)"), w_stage[:, 1:4:2, :])
+        nc.vector.tensor_copy(w_planes[64:128, 0, :], w_planes[0:64, 1, :])
+        w_plane_pair = w_planes[:, 0, :].bitcast(U8)
         a_scales = gather("a_scales", xt_plane, lists["offs"], U8)
-        a_words = gather("a_words", xt_tab, lists["offs"], U32)
+        w_sc = deal_scales("w_sc", w_plane_pair[:, 0:R])
+        a_words = gather("a_words", xt_tab, lists["offs"], U32, 0)
         a_banks = first_stage(0, w_dealt, w_sc, a_words, a_scales, E5M2)
 
         w2_dealt = deal_words("w2_dealt", w2_raw)
-        spread([(xo_plane, xo_stage), (w2_plane, w2_stage)])
-        w2_sc = deal_scales("w2_sc", w2_plane)
+        w2_sc = deal_scales("w2_sc", w_plane_pair[:, R : 2 * R])
         b_scales = gather("b_scales", xo_plane, lists["offs2"], U8)
         b_words = gather("b_words", xo_tab, lists["offs2"], U32)
         b_banks = first_stage(4, w2_dealt, w2_sc, b_words, b_scales, E4M3)
@@ -147,15 +146,18 @@ def tile_list_weighedboth_twotab_further_plain_kernel(tc, xt_words, xt_scales, w
         diff = tile("diff", [P, 4, O], F32)
         for t in range(4):
             rows = tile("a_rows%d" % t, [P, J], F32)
-            nc.scalar.activation(rows[:], a_banks[t][:], ACT.Copy)
+            if t < 2:
+                nc.scalar.activation(rows[:], a_banks[t][:], ACT.Copy)
+            else:
+                nc.vector.tensor_copy(rows[:], a_banks[t][:])
             nc.scalar.activation(a_picked[:, t, :], rows[:].indirect(lists["offs3"][:]), ACT.Copy, scale=sa_sb[:, t : t + 1])
 
-        s_scales = gather("s_scales", xt_plane, lists["offs5"], U8)
+        s_scales = gather("s_scales", xt_plane, lists["offs5"], U8, 0)
         for t in range(4):
             rows = tile("b_rows%d" % t, [P, J], F32)
             nc.vector.tensor_copy(rows[:], b_banks[t][:])
             nc.scalar.activation(b_picked[:, t, :], rows[:].indirect(lists["offs4"][:]), ACT.Copy, scale=sb_sb[:, t : t + 1])
-        s_words = gather("s_words", xt_tab, lists["offs5"], U32)
+        s_words = gather("s_words", xt_tab, lists["offs5"], U32, 128)
         for t in range(4):
             nc.vector.tensor_tensor(diff[:, t, :], a_picked[:, t, :], b_picked[:, t, :], ALU.subtract)
 
@@ -175,8 +177,12 @@ def tile_list_weighedboth_twotab_further_plain_kernel(tc, xt_words, xt_scales, w
 
         hid = tile("hid", [P, O, 4], BF16)
         woven = diff[:].rearrange("p t o -> p o t")
-        half = O // 2
-        nc.scalar.activation(hid[:, 0:half, :], woven[:, 0:half, :], ACT.Abs)
+        half = 88
+        nc.scalar.activation(
+            hid[:, 0:half, :].rearrange("p (c i) t -> p c t i", i=4),
+            diff[:, :, 0:half].rearrange("p t (c i) -> p c t i", i=4),
+            ACT.Abs,
+        )
         nc.vector.scalar_tensor_tensor(hid[:, half:O, :], woven[:, half:O, :], -1.0, woven[:, half:O, :], ALU.mult, ALU.max)
         hid_words = tile("hid_words", [P, O], U32)
         hid_scales = tile("hid_scales", [P, O], U8)

@@ -38,8 +38,8 @@ def tile_list_weighedboth_twotab_further_plain_kernel(tc, xt_words, xt_scales, w
             lists[name] = tile(name, list(src.shape), U16)
             nc.sync.dma_start(lists[name][:], src)
 
-        def load_words(queue, name, src, dtype):
-            words = tile(name, [P, src.shape[1] * 4 // {U32: 4, U8: 1}[dtype]], dtype)
+        def load_words(queue, name, src, dtype, offset=None):
+            words = tile(name, [P, src.shape[1] * 4 // {U32: 4, U8: 1}[dtype]], dtype, offset)
             queue.dma_start(words[:].bitcast(I32), src)
             return words
 
@@ -53,21 +53,13 @@ def tile_list_weighedboth_twotab_further_plain_kernel(tc, xt_words, xt_scales, w
                 src[0].bitcast(I32).rearrange("(q r) c -> r q c", q=4),
             )
 
-        def deal_scales(name, plane):
-            dealt = tile(name, [P, R], U8)
-            nc.vector.tensor_copy(
-                dealt[:].rearrange("p (t q) -> p t q", t=4),
-                plane.rearrange("p (q t) -> p t q", t=4),
-            )
-            return dealt
-
-        def deal_words(name, raw):
-            dealt = tile(name, [P, 2 * R], U8)
-            nc.scalar.copy(
-                dealt[:].bitcast(U16).rearrange("p (t q) -> p t q", t=4),
-                raw[:].bitcast(U16).rearrange("p (q t) -> p t q", t=4),
-            )
-            return dealt
+        def deal(engine_copy, name, columns, dtype, step):
+            slices = []
+            for first in range(0, 4, step):
+                dealt = tile("%s%d" % (name, first), [P, step, P], dtype)
+                engine_copy(dealt[:], columns.rearrange("p (q t) -> p t q", t=4)[:, first : first + step, :])
+                slices.extend(dealt[:, s, :] for s in range(step))
+            return slices
 
         def gather(name, table, offsets, dtype, offset=None):
             picked = tile(name, [P, 16 * offsets.shape[1]], dtype, offset)
@@ -76,7 +68,7 @@ def tile_list_weighedboth_twotab_further_plain_kernel(tc, xt_words, xt_scales, w
 
         xt_plane = tile("xt_plane", [P, T], U8)
         xo_plane = tile("xo_plane", [P, T], U8)
-        w_stage = tile("w_stage", [4, 4, 2 * R // 4], I32)
+        w_stage = tile("w_stage", [4, 2, 4, R // 4], I32)
         w_planes = tile("w_planes", [P, 2, 2 * R // 4], I32)
         ws_plane = tile("ws_plane", [P, N], U8)
         wb_plane = tile("wb_plane", [P, N], U8)
@@ -87,14 +79,14 @@ def tile_list_weighedboth_twotab_further_plain_kernel(tc, xt_words, xt_scales, w
             nc.vector.memset(plane[:].bitcast(I32), 0)
 
         table_view = "p c t -> p (c t)"
+        load_staged(nc.sync, w_stage[:, 0], w_scales)
+        load_staged(nc.sync, w_stage[:, 1], w2_scales)
         load_list("offs", offs)
-        load_staged(nc.sync, w_stage[:, :, 0 : R // 4], w_scales)
-        load_staged(nc.sync, w_stage[:, :, R // 4 : R // 2], w2_scales)
         load_plane(nc.sync, xt_plane, xt_scales)
         xt_tab = load_words(nc.sync, "xt_tab", xt_words[0].rearrange(table_view).bitcast(I32), U32)
         xo_tab = load_words(nc.sync, "xo_tab", xo_words[0].rearrange(table_view).bitcast(I32), U32)
         w_raw = load_words(nc.gpsimd, "w_raw", w_words[0].bitcast(I32), U8)
-        w2_raw = load_words(nc.gpsimd, "w2_raw", w2_words[0].bitcast(I32), U8)
+        w2_raw = load_words(nc.gpsimd, "w2_raw", w2_words[0].bitcast(I32), U8, 0)
         load_list("offs2", offs2)
         load_list("offs3", offs3)
         load_plane(nc.sync, xo_plane, xo_scales)
@@ -115,8 +107,8 @@ def tile_list_weighedboth_twotab_further_plain_kernel(tc, xt_words, xt_scales, w
                 bank = psum.tile([P, J], F32, name="bank%d" % (bank0 + t))
                 nc.tensor.matmul_mx(
                     out=bank[:],
-                    lhsT=weights[:, 2 * P * t : 2 * P * (t + 1)].bitcast(E2M1),
-                    lhsT_scale=weight_scales[:, P * t : P * (t + 1)],
+                    lhsT=weights[t].bitcast(E2M1),
+                    lhsT_scale=weight_scales[t],
                     rhs=words[:].bitcast(fmt),
                     rhs_scale=scales[:],
                     start=True,
@@ -125,41 +117,41 @@ def tile_list_weighedboth_twotab_further_plain_kernel(tc, xt_words, xt_scales, w
                 banks.append(bank)
             return banks
 
-        w_dealt = deal_words("w_dealt", w_raw)
-        nc.vector.tensor_copy(w_planes[0:4], w_stage[:, 0:4:2, :])
-        nc.vector.tensor_copy(w_planes[32:36].rearrange("p a c -> p (a c)"), w_stage[:, 1:4:2, :])
+        by_parity = w_stage[:].rearrange("r w (a b) c -> r b a w c", b=2)
+        nc.vector.tensor_copy(w_planes[0:4].rearrange("p a c -> p (a c)"), by_parity[:, 0])
+        nc.vector.tensor_copy(w_planes[32:36].rearrange("p a c -> p (a c)"), by_parity[:, 1])
         nc.vector.tensor_copy(w_planes[64:128, 0, :], w_planes[0:64, 1, :])
-        w_plane_pair = w_planes[:, 0, :].bitcast(U8)
         a_scales = gather("a_scales", xt_plane, lists["offs"], U8)
-        w_sc = deal_scales("w_sc", w_plane_pair[:, 0:R])
-        a_words = gather("a_words", xt_tab, lists["offs"], U32, 0)
+        w_plane_pair = w_planes[:, 0, :].bitcast(U8)
+        w_dealt = deal(nc.scalar.copy, "w_dealt", w_raw[:].bitcast(U16), U16, 2)
+        w_sc = deal(nc.vector.tensor_copy, "w_sc", w_plane_pair[:, 0:R], U8, 4)
+        a_words = gather("a_words", xt_tab, lists["offs"], U32)
         a_banks = first_stage(0, w_dealt, w_sc, a_words, a_scales, E5M2)
 
-        w2_dealt = deal_words("w2_dealt", w2_raw)
-        w2_sc = deal_scales("w2_sc", w_plane_pair[:, R : 2 * R])
+        w2_dealt = deal(nc.scalar.copy, "w2_dealt", w2_raw[:].bitcast(U16), U16, 4)
+        w2_sc = deal(nc.vector.tensor_copy, "w2_sc", w_plane_pair[:, R : 2 * R], U8, 4)
         b_scales = gather("b_scales", xo_plane, lists["offs2"], U8)
         b_words = gather("b_words", xo_tab, lists["offs2"], U32)
         b_banks = first_stage(4, w2_dealt, w2_sc, b_words, b_scales, E4M3)
 
         a_picked = tile("a_picked", [P, 4, O], F32)
-        b_picked = tile("b_picked", [P, 4, O], F32)
+        b_picked = tile("b_picked", [P, 4, O], F32, 1024)
         diff = tile("diff", [P, 4, O], F32)
         for t in range(4):
-            rows = tile("a_rows%d" % t, [P, J], F32)
+            rows = tile("a_rows%d" % t, [P, J], F32, 0 if t == 0 else None)
             if t < 2:
                 nc.scalar.activation(rows[:], a_banks[t][:], ACT.Copy)
             else:
                 nc.vector.tensor_copy(rows[:], a_banks[t][:])
             nc.scalar.activation(a_picked[:, t, :], rows[:].indirect(lists["offs3"][:]), ACT.Copy, scale=sa_sb[:, t : t + 1])
-
-        s_scales = gather("s_scales", xt_plane, lists["offs5"], U8, 0)
         for t in range(4):
             rows = tile("b_rows%d" % t, [P, J], F32)
             nc.vector.tensor_copy(rows[:], b_banks[t][:])
             nc.scalar.activation(b_picked[:, t, :], rows[:].indirect(lists["offs4"][:]), ACT.Copy, scale=sb_sb[:, t : t + 1])
-        s_words = gather("s_words", xt_tab, lists["offs5"], U32, 128)
         for t in range(4):
             nc.vector.tensor_tensor(diff[:, t, :], a_picked[:, t, :], b_picked[:, t, :], ALU.subtract)
+        s_scales = gather("s_scales", xt_plane, lists["offs5"], U8, 1024)
+        s_words = gather("s_words", xt_tab, lists["offs5"], U32, 1152)
 
         y_banks = []
         for h in range(2):
@@ -176,14 +168,11 @@ def tile_list_weighedboth_twotab_further_plain_kernel(tc, xt_words, xt_scales, w
             y_banks.append(bank)
 
         hid = tile("hid", [P, O, 4], BF16)
-        woven = diff[:].rearrange("p t o -> p o t")
-        half = 88
         nc.scalar.activation(
-            hid[:, 0:half, :].rearrange("p (c i) t -> p c t i", i=4),
-            diff[:, :, 0:half].rearrange("p t (c i) -> p c t i", i=4),
+            hid[:].rearrange("p (c i) t -> p c t i", i=4),
+            diff[:].rearrange("p t (c i) -> p c t i", i=4),
             ACT.Abs,
         )
-        nc.vector.scalar_tensor_tensor(hid[:, half:O, :], woven[:, half:O, :], -1.0, woven[:, half:O, :], ALU.mult, ALU.max)
         hid_words = tile("hid_words", [P, O], U32)
         hid_scales = tile("hid_scales", [P, O], U8)
         nc.vector.quantize_mx(out=hid_words[:].bitcast(E4M3), scales=hid_scales[:], in_=hid[:].rearrange("p o t -> p (o t)"))

@@ -84,16 +84,16 @@ def tile_list_weighedboth_twotab_further_plain_kernel(tc, xt_words, xt_scales, w
         load_list("offs", offs)
         load_plane(nc.sync, xt_plane, xt_scales)
         xt_tab = load_words(nc.sync, "xt_tab", xt_words[0].rearrange(table_view).bitcast(I32), U32)
-        xo_tab = load_words(nc.sync, "xo_tab", xo_words[0].rearrange(table_view).bitcast(I32), U32)
         w_raw = load_words(nc.gpsimd, "w_raw", w_words[0].bitcast(I32), U8)
         w2_raw = load_words(nc.gpsimd, "w2_raw", w2_words[0].bitcast(I32), U8, 0)
         load_list("offs2", offs2)
         load_list("offs3", offs3)
+        xo_tab = load_words(nc.sync, "xo_tab", xo_words[0].rearrange(table_view).bitcast(I32), U32)
         load_plane(nc.sync, xo_plane, xo_scales)
         sa_sb = tile("sa_sb", [P, 4], F32)
-        nc.sync.dma_start(sa_sb[:], sa.rearrange("(p t) o -> p (t o)", t=4))
+        nc.gpsimd.dma_start(sa_sb[:], sa.rearrange("(p t) o -> p (t o)", t=4))
         sb_sb = tile("sb_sb", [P, 4], F32)
-        nc.sync.dma_start(sb_sb[:], sb.rearrange("(p t) o -> p (t o)", t=4))
+        nc.gpsimd.dma_start(sb_sb[:], sb.rearrange("(p t) o -> p (t o)", t=4))
         load_list("offs4", offs4)
         load_list("offs5", offs5)
         ws_w = load_words(nc.gpsimd, "ws_w", ws_words[0].bitcast(I32), U8)

from contextlib import ExitStack

import concourse.mybir as mybir

K, T, J, R, O, N = 512, 1024, 256, 512, 128, 256
FLOPS = 2 * K * R * J * 2 + 2 * R * N * O * 2

F32 = mybir.dt.float32
BF16 = mybir.dt.bfloat16
I32 = mybir.dt.int32
U32 = mybir.dt.uint32
U16 = mybir.dt.uint16
U8 = mybir.dt.uint8
E4M3 = mybir.dt.float8_e4m3fn_x4
E5M2 = mybir.dt.float8_e5m2_x4
E2M1 = mybir.dt.float4_e2m1fn_x4
ALU = mybir.AluOpType
ACT = mybir.ActivationFunctionType
P = 128


def tile_list_weighedboth_twotab_further_plain_kernel(tc, xt_words, xt_scales, w_words, w_scales, xo_words, xo_scales, w2_words, w2_scales, sa, sb, wb_words, wb_scales, ws_words, ws_scales, offs, offs2, offs3, offs4, offs5, out):
    nc = tc.nc
    with ExitStack() as ctx:
        sbuf = ctx.enter_context(tc.tile_pool(name="sbuf", bufs=1))
        psum = ctx.enter_context(tc.psum_pool(name="psum", bufs=1))

        reused = ctx.enter_context(tc.tile_pool(name="reused", bufs=1))

        def tile(name, shape, dtype, offset=None):
            if offset is None:
                return sbuf.tile(shape, dtype, name=name, align_bytes=64)
            return reused.tile(shape, dtype, name=name, align_bytes=64, offset=offset)

        lists = {}

        def load_list(name, src):
            lists[name] = tile(name, list(src.shape), U16)
            nc.sync.dma_start(lists[name][:], src)

        def load_words(queue, name, src, dtype, offset=None):
            words = tile(name, [P, src.shape[1] * 4 // {U32: 4, U8: 1}[dtype]], dtype, offset)
            queue.dma_start(words[:].bitcast(I32), src)
            return words

        def load_plane(queue, plane, src):
            for q in range(4):
                queue.dma_start(plane[32 * q : 32 * q + 4, :].bitcast(I32), src[0, 4 * q : 4 * q + 4, :].bitcast(I32))

        def load_staged(queue, stage, src):
            queue.dma_start(
                stage,
                src[0].bitcast(I32).rearrange("(q r) c -> r q c", q=4),
            )

        def deal(engine_copy, name, columns, dtype, step):
            slices = []
            for first in range(0, 4, step):
                dealt = tile("%s%d" % (name, first), [P, step, P], dtype)
                engine_copy(dealt[:], columns.rearrange("p (q t) -> p t q", t=4)[:, first : first + step, :])
                slices.extend(dealt[:, s, :] for s in range(step))
            return slices

        def gather(name, table, offsets, dtype, offset=None):
            picked = tile(name, [P, 16 * offsets.shape[1]], dtype, offset)
            nc.vector.tensor_copy(picked[:], table[:].indirect(offsets[:]))
            return picked

        xt_plane = tile("xt_plane", [P, T], U8)
        xo_plane = tile("xo_plane", [P, T], U8)
        w_stage = tile("w_stage", [4, 2, 4, R // 4], I32)
        w_planes = tile("w_planes", [P, 2, 2 * R // 4], I32)
        ws_plane = tile("ws_plane", [P, N], U8)
        wb_plane = tile("wb_plane", [P, N], U8)
        nc.gpsimd.memset(xt_plane[:].bitcast(I32), 0)
        nc.vector.memset(xo_plane[:].bitcast(I32), 0)
        nc.vector.memset(w_planes[0:64], 0)
        for plane in (ws_plane, wb_plane):
            nc.vector.memset(plane[:].bitcast(I32), 0)

        table_view = "p c t -> p (c t)"
        load_staged(nc.sync, w_stage[:, 0], w_scales)
        load_staged(nc.sync, w_stage[:, 1], w2_scales)
        load_list("offs", offs)
        load_plane(nc.sync, xt_plane, xt_scales)
        xt_tab = load_words(nc.sync, "xt_tab", xt_words[0].rearrange(table_view).bitcast(I32), U32)
        w_raw = load_words(nc.gpsimd, "w_raw", w_words[0].bitcast(I32), U8)
        w2_raw = load_words(nc.gpsimd, "w2_raw", w2_words[0].bitcast(I32), U8, 0)
        load_list("offs2", offs2)
        load_list("offs3", offs3)
        xo_tab = load_words(nc.sync, "xo_tab", xo_words[0].rearrange(table_view).bitcast(I32), U32)
        load_plane(nc.sync, xo_plane, xo_scales)
        sa_sb = tile("sa_sb", [P, 4], F32)
        nc.gpsimd.dma_start(sa_sb[:], sa.rearrange("(p t) o -> p (t o)", t=4))
        sb_sb = tile("sb_sb", [P, 4], F32)
        nc.gpsimd.dma_start(sb_sb[:], sb.rearrange("(p t) o -> p (t o)", t=4))
        load_list("offs4", offs4)
        load_list("offs5", offs5)
        ws_w = load_words(nc.gpsimd, "ws_w", ws_words[0].bitcast(I32), U8)
        wb_w = load_words(nc.gpsimd, "wb_w", wb_words[0].bitcast(I32), U8)
        load_plane(nc.sync, ws_plane, ws_scales)
        load_plane(nc.sync, wb_plane, wb_scales)

        def first_stage(bank0, weights, weight_scales, words, scales, fmt):
            banks = []
            for t in range(4):
                bank = psum.tile([P, J], F32, name="bank%d" % (bank0 + t))
                nc.tensor.matmul_mx(
                    out=bank[:],
                    lhsT=weights[t].bitcast(E2M1),
                    lhsT_scale=weight_scales[t],
                    rhs=words[:].bitcast(fmt),
                    rhs_scale=scales[:],
                    start=True,
                    stop=True,
                )
                banks.append(bank)
            return banks

        by_parity = w_stage[:].rearrange("r w (a b) c -> r b a w c", b=2)
        nc.vector.tensor_copy(w_planes[0:4].rearrange("p a c -> p (a c)"), by_parity[:, 0])
        nc.vector.tensor_copy(w_planes[32:36].rearrange("p a c -> p (a c)"), by_parity[:, 1])
        nc.vector.tensor_copy(w_planes[64:128, 0, :], w_planes[0:64, 1, :])
        a_scales = gather("a_scales", xt_plane, lists["offs"], U8)
        w_plane_pair = w_planes[:, 0, :].bitcast(U8)
        w_dealt = deal(nc.scalar.copy, "w_dealt", w_raw[:].bitcast(U16), U16, 2)
        w_sc = deal(nc.vector.tensor_copy, "w_sc", w_plane_pair[:, 0:R], U8, 4)
        a_words = gather("a_words", xt_tab, lists["offs"], U32)
        a_banks = first_stage(0, w_dealt, w_sc, a_words, a_scales, E5M2)

        w2_dealt = deal(nc.scalar.copy, "w2_dealt", w2_raw[:].bitcast(U16), U16, 4)
        w2_sc = deal(nc.vector.tensor_copy, "w2_sc", w_plane_pair[:, R : 2 * R], U8, 4)
        b_scales = gather("b_scales", xo_plane, lists["offs2"], U8)
        b_words = gather("b_words", xo_tab, lists["offs2"], U32)
        b_banks = first_stage(4, w2_dealt, w2_sc, b_words, b_scales, E4M3)

        a_picked = tile("a_picked", [P, 4, O], F32)
        b_picked = tile("b_picked", [P, 4, O], F32, 1024)
        diff = tile("diff", [P, 4, O], F32)
        for t in range(4):
            rows = tile("a_rows%d" % t, [P, J], F32, 0 if t == 0 else None)
            if t < 2:
                nc.scalar.activation(rows[:], a_banks[t][:], ACT.Copy)
            else:
                nc.vector.tensor_copy(rows[:], a_banks[t][:])
            nc.scalar.activation(a_picked[:, t, :], rows[:].indirect(lists["offs3"][:]), ACT.Copy, scale=sa_sb[:, t : t + 1])
        for t in range(4):
            rows = tile("b_rows%d" % t, [P, J], F32)
            nc.vector.tensor_copy(rows[:], b_banks[t][:])
            nc.scalar.activation(b_picked[:, t, :], rows[:].indirect(lists["offs4"][:]), ACT.Copy, scale=sb_sb[:, t : t + 1])
        for t in range(4):
            nc.vector.tensor_tensor(diff[:, t, :], a_picked[:, t, :], b_picked[:, t, :], ALU.subtract)
        s_scales = gather("s_scales", xt_plane, lists["offs5"], U8, 1024)
        s_words = gather("s_words", xt_tab, lists["offs5"], U32, 1152)

        y_banks = []
        for h in range(2):
            bank = psum.tile([P, O], F32, name="bank%d" % h)
            nc.tensor.matmul_mx(
                out=bank[:],
                lhsT=ws_w[:, 2 * P * h : 2 * P * (h + 1)].bitcast(E2M1),
                lhsT_scale=ws_plane[:, P * h : P * (h + 1)],
                rhs=s_words[:].bitcast(E5M2),
                rhs_scale=s_scales[:],
                start=True,
                stop=False,
            )
            y_banks.append(bank)

        hid = tile("hid", [P, O, 4], BF16)
        nc.scalar.activation(
            hid[:].rearrange("p (c i) t -> p c t i", i=4),
            diff[:].rearrange("p t (c i) -> p c t i", i=4),
            ACT.Abs,
        )
        hid_words = tile("hid_words", [P, O], U32)
        hid_scales = tile("hid_scales", [P, O], U8)
        nc.vector.quantize_mx(out=hid_words[:].bitcast(E4M3), scales=hid_scales[:], in_=hid[:].rearrange("p o t -> p (o t)"))

        for h in range(2):
            nc.tensor.matmul_mx(
                out=y_banks[h][:],
                lhsT=wb_w[:, 2 * P * h : 2 * P * (h + 1)].bitcast(E2M1),
                lhsT_scale=wb_plane[:, P * h : P * (h + 1)],
                rhs=hid_words[:].bitcast(E4M3),
                rhs_scale=hid_scales[:],
                start=False,
                stop=True,
            )
        y0 = tile("y0", [P, O], F32)
        y1 = tile("y1", [P, O], F32)
        nc.vector.tensor_copy(y0[:], y_banks[0][:])
        nc.sync.dma_start(out[0:P, :], y0[:])
        nc.scalar.copy(y1[:], y_banks[1][:])
        nc.scalar.dma_start(out[P : 2 * P, :], y1[:])
